import numpy as np, ml_dtypes
CORES = [32,33,34,35,40,41,42,43]
N = 8
def setup_inputs(rng):
    return {"x": rng.standard_normal((N, 128, 256), dtype=np.float32).astype(ml_dtypes.bfloat16)}
def reference(x):
    g = np.ascontiguousarray(x.transpose(1, 2, 0)).reshape(128, 256 * N)
    return {"y": np.broadcast_to(g, (N,) + g.shape)}

import comms_topo
from concourse.bass import DstId, RemoteDMATransfer

RANKS = (32, 33, 34, 35, 40, 41, 42, 43)
NCORES = 48
CHIP_ORDER = (4, 0, 2, 5, 1, 3)


def is_port(c):
    return c % 8 in (2, 3, 6, 7)


def par(c):
    return (c // 8) & 1


def units_of(c):
    return 6 if (c // 8 < 4 and is_port(c)) else 5


CLASSES = (6, 5)
MEMBERS = {}
SLOT = {}
BASE = {}


def build_tables():
    u0 = 0
    for U in CLASSES:
        m = [c for ch in CHIP_ORDER for c in range(8 * ch, 8 * ch + 8) if units_of(c) == U]
        MEMBERS[U] = m
        BASE[U] = u0
        for k, c in enumerate(m):
            SLOT[c] = k
        u0 += U * len(m)
    assert u0 == 256


build_tables()

SCRATCH = {}
for U_ in CLASSES:
    K_ = len(MEMBERS[U_])
    SCRATCH["xs%d" % U_] = ("dram", [K_, 128, U_], "bfloat16")
    SCRATCH["rl%d" % U_] = ("dram", [K_, 128, U_], "bfloat16")
    SCRATCH["land%d" % U_] = ("dram", [8, 128, U_], "bfloat16")
    SCRATCH["out%d" % U_] = ("dram", [128, 8 * U_], "bfloat16")
    SCRATCH["rel%d" % U_] = ("dram", [128, 8 * U_], "bfloat16")
    SCRATCH["gat%d" % U_] = ("dram", [K_, 128, 8 * U_], "bfloat16")

SEMAPHORES = (["ld", "il", "own", "yd", "snt"] + ["a%d" % r for r in range(8)] + ["q%d" % U_ for U_ in CLASSES]
              + ["r%d" % w for w in range(NCORES)])


def bits(m):
    return bin(m).count("1")


def forwarder(w):
    return w + 2


def result_plan(w):
    same = [q for q in RANKS if par(q) == par(w) and q != w]
    cross = [q for q in RANKS if par(q) != par(w)]
    if is_port(w):
        d = same + cross
    else:
        d = same + ([] if forwarder(w) in same else [forwarder(w)])
    on = [q for q in d if q // 8 == w // 8]
    off = [q for q in d if q // 8 != w // 8]
    if on and off:
        return [(0xFF00, on), (0x00FF, off)]
    if on:
        return [(0xFFFF, on)]
    return [(0x00FF, off)]


def result_inc(dst, w):
    for m, d in result_plan(w):
        if dst in d:
            return bits(m)
    return 8


def pack(core, items):
    off = [i for i in items if i[0] // 8 != core // 8]
    on = [i for i in items if i[0] // 8 == core // 8]
    calls = []
    while off or on:
        cur = []
        for it in off[:8]:
            cur.append((1 << len(cur), it[1], [(it[0], it[2])], it[3]))
        off = off[8:]
        n = 16 - len(cur)
        for it in on[:n]:
            cur.append((1 << len(cur), it[1], [(it[0], it[2])], it[3]))
        on = on[n:]
        calls.append(cur)
    return calls


def source_order(core):
    own = [r for r in range(8) if RANKS[r] == core]
    same = [r for r in range(8) if par(RANKS[r]) == par(core) and RANKS[r] != core]
    cp = [r for r in range(8) if par(RANKS[r]) != par(core) and is_port(RANKS[r])]
    cr = [r for r in range(8) if par(RANKS[r]) != par(core) and not is_port(RANKS[r])]
    return own + same + cp + cr


def rank_program(g, core, T, topo):
    rank = T.rank_of(core)
    U = units_of(core)
    k = SLOT[core]
    sent = [0]

    def did(c):
        a = topo.addr(c)
        return DstId(rid=a[0], pnc=a[1])

    def call(items):
        tr = []
        for mask, src, dl, sem in items:
            tr.append(RemoteDMATransfer(dst_ids=[did(d[0]) for d in dl], dma_engine_mask=mask,
                                        remote_sem=T.sem[sem], srcs=[src], dsts=[d[1] for d in dl]))
            sent[0] += bits(mask)
        g.remote_dma_fused(tr, local_sem=T.sem.snt)

    if rank is not None:
        for i, C in enumerate(CLASSES):
            q = g.sync if i % 2 == 0 else g.scalar
            r0 = BASE[C] // 2
            r1 = r0 + C * len(MEMBERS[C]) // 2
            q.dma_start(T["xs%d" % C][:], T.x[r0:r1, :]).then_inc(T.sem.ld, 16)
        g.wait_ge(T.sem.ld, 16 * len(CLASSES))
        for C in CLASSES:
            items = []
            late = []
            for w in MEMBERS[C]:
                if w == core:
                    continue
                s = SLOT[w]
                if topo.may_write(core, w):
                    items.append((w, T["xs%d" % C][s], T["land%d" % C][rank], "a%d" % rank))
                else:
                    late.append((core + 6, T["xs%d" % C][s], T["rl%d" % C][s], "q%d" % C))
            for c in pack(core, items + late):
                call(c)

    if (core - 6) in RANKS and not is_port(core - 6):
        rr = RANKS.index(core - 6)
        for C in CLASSES:
            ws = [w for w in MEMBERS[C] if par(w) != par(core)]
            g.wait_ge(T.sem["q%d" % C], len(ws))
            items = [(w, T["rl%d" % C][SLOT[w]], T["land%d" % C][rr], "a%d" % rr) for w in ws]
            for c in pack(core, items):
                call(c)

    for r in source_order(core):
        if RANKS[r] == core:
            src = T["xs%d" % U][k]
        else:
            g.wait_ge(T.sem["a%d" % r], 1)
            src = T["land%d" % U][r]
        if rank is not None:
            dst = T["gat%d" % U][k, :, r:8 * U:8]
        else:
            dst = T["out%d" % U][:, r:8 * U:8]
        g.dma_start(dst, src, allow_slow_non_contiguous=True).then_inc(T.sem.il, 16)
    g.wait_ge(T.sem.il, 16 * 8)
    if rank is not None:
        g.sem_inc(T.sem.own, 1)

    mine = T["gat%d" % U][k] if rank is not None else T["out%d" % U][:]

    def landing(d, w):
        C = units_of(w)
        return T["gat%d" % C][SLOT[w]] if d in RANKS else T["rel%d" % C][:]

    call([(m, mine, [(d, landing(d, core)) for d in dl], "r%d" % core) for m, dl in result_plan(core)])
    if is_port(core):
        w = core - 2
        g.wait_ge(T.sem["r%d" % w], result_inc(core, w))
        cross = [q for q in RANKS if par(q) != par(core)]
        call([(0x00FF, landing(core, w), [(d, landing(d, w)) for d in cross], "r%d" % w)])

    if rank is not None:
        n = 0
        for p in (par(core), 1 - par(core)):
            for i, C in enumerate(CLASSES):
                q = g.sync if i % 2 == 1 else g.scalar
                ws = [w for w in MEMBERS[C] if par(w) == p]
                k0 = SLOT[ws[0]]
                k1 = SLOT[ws[-1]] + 1
                assert k1 - k0 == len(ws)
                r0 = (BASE[C] + k0 * C) // 2
                r1 = (BASE[C] + k1 * C) // 2
                for w in ws:
                    if w == core:
                        q.wait_ge(T.sem.own, 1)
                    else:
                        q.wait_ge(T.sem["r%d" % w], result_inc(core, w))
                q.dma_start(T.y[r0:r1, :], T["gat%d" % C][k0:k1]).then_inc(T.sem.yd, 16)
                n += 1
        g.wait_ge(T.sem.yd, 16 * n)

    g.wait_ge(T.sem.snt, sent[0])
